import numpy as np, ml_dtypes
CORES = [10,34,74,98]
N = 4
import mx_ref
NC, G = 128, 4
EPS = 0.001
BF = ml_dtypes.bfloat16
def cut(t, i, w=512):
    return t[:, w * i:w * i + w]
def tile(rs):
    return np.stack(rs, axis=2).reshape(128, -1).astype(BF)
def layer(w, X):
    out = []
    for i in range(G):
        for t in range(len(X)):
            p = mx_ref.matmul(mx_ref.quantize(cut(w, len(X) * i + t)), X[t])
            z = p if t == 0 else z + p
        out.append(z)
    return out
def setup_inputs(rng):
    def f(*shape):
        return mx_ref.flush((rng.standard_normal(shape, dtype=np.float32) * np.exp2(rng.integers(-2, 3, shape[:-1] + (1,)))).astype(BF))
    return {"x": f(N, 128, 4 * NC), "w1": f(N, 128, G * 512), "w2": f(N, 128, 2 * 512)}
def setup_inputs_blocks(rng):
    d = setup_inputs(rng)
    for k in ("x", "w1", "w2"): d[k] = mx_ref.spread(d[k], rng, 4)
    return d
def setup_inputs_wide(rng):
    d = setup_inputs(rng)
    for k in ("x", "w1", "w2"): d[k] = mx_ref.flush((d[k].astype(np.float32) * np.exp2(rng.integers(-6, 7, (N, 1, 1))).astype(np.float32)).astype(BF))
    return d
def setup_inputs_cols(rng):
    d = setup_inputs(rng); v = d["x"].astype(np.float32).reshape(N, 128, -1, 4)
    d["x"] = mx_ref.flush((v * np.exp2(rng.integers(-6, 7, (N, 1, v.shape[2], 1))).astype(np.float32)).reshape(d["x"].shape).astype(BF))
    return d
def setup_inputs_faint(rng):
    d = setup_inputs(rng); d["x"] = mx_ref.flush((d["x"].astype(np.float32) * np.float32(2.0 ** -12)).astype(BF))
    return d
def reference(x, w1, w2, own=None):
    h = np.zeros((N, 128, 4 * NC), BF)
    for r in range(N):
        Z = layer(w1[r], [mx_ref.quantize(x[r])]); R = Z
        ms = sum((v.astype(np.float64) ** 2).sum(axis=0) for v in R) / 512
        s = (1 / np.sqrt(ms + EPS)).astype(np.float32)
        h[r] = tile([v * s for v in R])
    use = h if own is None else own["h"]
    H = [mx_ref.quantize(use[j]) for j in range(N)]
    y = np.zeros((N, 128, NC), np.float32)
    for r in range(N):
        y[r] = mx_ref.matmul(mx_ref.quantize(cut(w2[r], 0)), H[r]) + mx_ref.matmul(mx_ref.quantize(cut(w2[r], 1)), H[(r + 1) % N])
    return {"h": h, "y": y}

@@ -1,0 +1,165 @@
+from concourse.mybir import dt, AluOpType, ActivationFunctionType
+
+NC = 128
+TW = 4 * NC
+G = 4
+EPS = 0.001
+
+SCRATCH = {
+    "xb": ("sbuf", [128, TW], "bfloat16"),
+    "w1b": ("sbuf", [128, G * TW], "bfloat16"),
+    "w2b": ("sbuf", [128, 2 * TW], "bfloat16"),
+    "xq": ("sbuf", [128, NC], "float8_e4m3fn_x4"),
+    "xs": ("sbuf", [128, NC], "uint8"),
+    "w1q": ("sbuf", [128, G * NC], "float8_e4m3fn_x4"),
+    "w1s": ("sbuf", [128, G * NC], "uint8"),
+    "w2q": ("sbuf", [128, 2 * NC], "float8_e4m3fn_x4"),
+    "w2s": ("sbuf", [128, 2 * NC], "uint8"),
+    "hb": ("sbuf", [128, TW], "bfloat16"),
+    "hq": ("sbuf", [128, NC], "float8_e4m3fn_x4"),
+    "hs": ("sbuf", [128, NC], "uint8"),
+    "rq": ("sbuf", [128, NC], "float8_e4m3fn_x4"),
+    "rs": ("sbuf", [128, NC], "uint8"),
+    "sqb": ("sbuf", [128, G * NC], "float32"),
+    "zcb": ("sbuf", [128, G * NC], "float32"),
+    "ones": ("sbuf", [128, 128], "float32"),
+    "ident": ("sbuf", [128, 128], "float32"),
+    "diag": ("sbuf", [128, 128], "float32"),
+    "cmean": ("sbuf", [128, 1], "float32"),
+    "ceps": ("sbuf", [128, 1], "float32"),
+    "rtb": ("sbuf", [128, 1], "float32"),
+    "y0b": ("sbuf", [128, 1], "float32"),
+    "nvb": ("sbuf", [128, 1], "float32"),
+    "nwb": ("sbuf", [128, 1], "float32"),
+    "yb": ("sbuf", [128, NC], "float32"),
+    "zp": ("psum", [128, G * 512], "float32"),
+    "stp": ("psum", [128, 512], "float32"),
+    "bcp": ("psum", [128, 512], "float32"),
+    "yp": ("psum", [128, 512], "float32"),
+}
+
+SEMAPHORES = (
+    ["ld_x", "ld_w2", "c_ones", "c_col", "c_id", "q_x", "q_h", "q_w2a", "q_w2b",
+     "e_cp", "e_st", "e_rt", "e_rc", "e_nv", "e_nw", "e_diag", "e_bc", "e_h", "issued", "sent", "arrived",
+     "e_y", "e_yb", "st_h", "st_y"]
+    + ["ld_w1_%d" % b for b in range(G)]
+    + ["q_w1_%d" % b for b in range(G)]
+    + ["mm_%d" % b for b in range(G)]
+    + ["sq_%d" % b for b in range(G)]
+)
+
+
+def rank_program(g, core, T, topo):
+    rank = T.rank_of(core)
+    if rank is None:
+        return
+    n = len(T.cores)
+    dst = T.cores[(rank - 1) % n]
+    if not topo.may_write(core, dst):
+        raise ValueError("core %d may not write to core %d" % (core, dst))
+    S = T.sem
+    V, PE, ACT, SY = g.vector, g.tensor, g.scalar, g.sync
+    mult, add = AluOpType.mult, AluOpType.add
+    AF = ActivationFunctionType
+
+    def cols(t, b, w):
+        return t[:, b * w:(b + 1) * w]
+
+    SY.dma_start(T.xb[:], T.x[:]).then_inc(S.ld_x, 16)
+    for b in range(G):
+        q = ACT if b % 2 == 0 else SY
+        q.dma_start(cols(T.w1b, b, TW), cols(T.w1, b, TW)).then_inc(S["ld_w1_%d" % b], 16)
+    SY.dma_start(T.w2b[:], T.w2[:]).then_inc(S.ld_w2, 16)
+
+    V.memset(T.ones[:], 1.0).then_inc(S.c_ones, 1)
+    V.memset(T.cmean[:], 1.0 / (G * 128)).then_inc(S.c_col, 1)
+    V.memset(T.ceps[:], EPS / 128).then_inc(S.c_col, 1)
+    g.wait_ge(S.c_ones, 1)
+    g.affine_select(T.ident[:], T.ones[:], [[-1, 128]], AluOpType.is_equal, 0.0, 0, 1).then_inc(S.c_id, 1)
+
+    V.wait_ge(S.ld_x, 16)
+    V.quantize_mx(T.xq[:], T.xs[:], T.xb[:]).then_inc(S.q_x, 1)
+    for b in range(G):
+        V.wait_ge(S["ld_w1_%d" % b], 16)
+        V.quantize_mx(cols(T.w1q, b, NC), cols(T.w1s, b, NC), cols(T.w1b, b, TW)).then_inc(S["q_w1_%d" % b], 1)
+
+    def product(b):
+        PE.wait_ge(S["q_w1_%d" % b], 1)
+        PE.matmul_mx(T.zp[:, 512 * b:512 * b + NC], cols(T.w1q, b, NC), cols(T.w1s, b, NC),
+                     T.xq[:], T.xs[:], True, True).then_inc(S["mm_%d" % b], 1)
+
+    def mean(b):
+        PE.wait_ge(S["sq_%d" % b], 1)
+        return PE.matmul(T.stp[:, 0:1], cols(T.sqb, b, NC), T.cmean[:], False, b == G - 1)
+
+    PE.wait_ge(S.c_ones, 1)
+    PE.wait_ge(S.c_col, 2)
+    PE.matmul(T.stp[:, 0:1], T.ones[:], T.ceps[:], True, False)
+    PE.wait_ge(S.q_x, 1)
+    product(0)
+    product(1)
+    mean(0)
+    product(2)
+    mean(1)
+    mean(2)
+    product(3)
+    mean(3).then_inc(S.e_st, 1)
+
+    for b in range(G):
+        zb = T.zp[:, 512 * b:512 * b + NC]
+        ACT.wait_ge(S["mm_%d" % b], 1)
+        ACT.activation(cols(T.sqb, b, NC), zb, AF.Square).then_inc(S["sq_%d" % b], 1)
+        ACT.activation(cols(T.zcb, b, NC), zb, AF.Copy).then_inc(S.e_cp, 1)
+    ACT.wait_ge(S.e_st, 1)
+    ACT.activation(T.rtb[:], T.stp[:, 0:1], AF.Sqrt).then_inc(S.e_rt, 1)
+
+    V.wait_ge(S.e_rt, 1)
+    V.reciprocal(T.y0b[:], T.rtb[:]).then_inc(S.e_rc, 1)
+    V.wait_ge(S.e_rc, 1)
+    V.tensor_scalar(T.nvb[:], T.stp[:, 0:1], T.y0b[:], T.y0b[:], mult, mult).then_inc(S.e_nv, 1)
+    V.wait_ge(S.e_nv, 1)
+    V.tensor_scalar(T.nwb[:], T.nvb[:], -0.5, 1.5, mult, add).then_inc(S.e_nw, 1)
+    V.wait_ge(S.e_nw, 1)
+    V.wait_ge(S.c_id, 1)
+    V.tensor_scalar(T.diag[:], T.ident[:], T.y0b[:], T.nwb[:], mult, mult).then_inc(S.e_diag, 1)
+
+    PE.wait_ge(S.e_diag, 1)
+    PE.matmul(T.bcp[:, 0:NC], T.ones[:], T.diag[:], True, True).then_inc(S.e_bc, 1)
+
+    V.wait_ge(S.e_bc, 1)
+    V.wait_ge(S.e_cp, G)
+    for b in range(G):
+        V.tensor_tensor(T.hb[:, b:TW:4], cols(T.zcb, b, NC), T.bcp[:, 0:NC], mult).then_inc(S.e_h, 1)
+    V.wait_ge(S.e_h, G)
+    V.quantize_mx(T.hq[:], T.hs[:], T.hb[:]).then_inc(S.q_h, 1)
+    V.wait_ge(S.ld_w2, 16)
+    V.quantize_mx(cols(T.w2q, 0, NC), cols(T.w2s, 0, NC), cols(T.w2b, 0, TW)).then_inc(S.q_w2a, 1)
+    V.quantize_mx(cols(T.w2q, 1, NC), cols(T.w2s, 1, NC), cols(T.w2b, 1, TW)).then_inc(S.q_w2b, 1)
+
+    rid, pid, _ = topo.addr(dst)
+    mask = topo.mask(core, dst)
+    engines = bin(mask).count("1")
+    g.wait_ge(S.q_h, 1)
+    g.remote_dma(T.rq[:].bitcast(dt.uint8), T.hq[:].bitcast(dt.uint8), S.arrived, S.sent, pid, rid, mask)
+    g.remote_dma(T.rs[:], T.hs[:], S.arrived, S.sent, pid, rid, mask)
+    g.sem_inc(S.issued, 1)
+    g.wait_ge(S.sent, 2 * engines)
+
+    SY.wait_ge(S.e_h, G)
+    SY.wait_ge(S.issued, 1)
+    SY.dma_start(T.h[:], T.hb[:]).then_inc(S.st_h, 16)
+
+    PE.wait_ge(S.q_h, 1)
+    PE.wait_ge(S.q_w2a, 1)
+    PE.matmul_mx(T.yp[:, 0:NC], cols(T.w2q, 0, NC), cols(T.w2s, 0, NC), T.hq[:], T.hs[:], True, False)
+    PE.wait_ge(S.q_w2b, 1)
+    src = T.cores[(rank + 1) % n]
+    PE.wait_ge(S.arrived, 2 * bin(topo.mask(src, core)).count("1"))
+    PE.matmul_mx(T.yp[:, 0:NC], cols(T.w2q, 1, NC), cols(T.w2s, 1, NC), T.rq[:], T.rs[:], False, True).then_inc(S.e_y, 1)
+
+    V.wait_ge(S.e_y, 1)
+    V.tensor_copy(T.yb[:], T.yp[:, 0:NC]).then_inc(S.e_yb, 1)
+    SY.wait_ge(S.e_yb, 1)
+    SY.dma_start(T.y[:], T.yb[:]).then_inc(S.st_y, 16)
+    SY.wait_ge(S.st_h, 16)
+    SY.wait_ge(S.st_y, 16)

@@ -4,6 +4,7 @@ NC = 128
 TW = 4 * NC
 G = 4
 EPS = 0.001
+SC = 2.0 ** -44
 
 SCRATCH = {
     "xb": ("sbuf", [128, TW], "bfloat16"),
@@ -23,14 +24,12 @@ SCRATCH = {
     "sqb": ("sbuf", [128, G * NC], "float32"),
     "zcb": ("sbuf", [128, G * NC], "float32"),
     "ones": ("sbuf", [128, 128], "float32"),
+    "back": ("sbuf", [128, 128], "float32"),
     "ident": ("sbuf", [128, 128], "float32"),
     "diag": ("sbuf", [128, 128], "float32"),
     "cmean": ("sbuf", [128, 1], "float32"),
     "ceps": ("sbuf", [128, 1], "float32"),
-    "rtb": ("sbuf", [128, 1], "float32"),
-    "y0b": ("sbuf", [128, 1], "float32"),
-    "nvb": ("sbuf", [128, 1], "float32"),
-    "nwb": ("sbuf", [128, 1], "float32"),
+    "tb": ("sbuf", [128, 1], "float32"),
     "yb": ("sbuf", [128, NC], "float32"),
     "zp": ("psum", [128, G * 512], "float32"),
     "stp": ("psum", [128, 512], "float32"),
@@ -39,9 +38,8 @@ SCRATCH = {
 }
 
 SEMAPHORES = (
-    ["ld_x", "ld_w2", "c_ones", "c_col", "c_id", "q_x", "q_h", "q_w2a", "q_w2b",
-     "e_cp", "e_st", "e_rt", "e_rc", "e_nv", "e_nw", "e_diag", "e_bc", "e_h", "issued", "sent", "arrived",
-     "e_y", "e_yb", "st_h", "st_y"]
+    ["ld_x", "ld_w2", "c_ones", "c_col", "c_id", "c_back", "q_x", "q_h", "q_w2a", "q_w2b",
+     "e_cp", "e_st", "e_rc", "e_diag", "e_bc", "e_h", "issued", "sent", "arrived", "e_y", "e_yb", "st_h", "st_y"]
     + ["ld_w1_%d" % b for b in range(G)]
     + ["q_w1_%d" % b for b in range(G)]
     + ["mm_%d" % b for b in range(G)]
@@ -59,7 +57,7 @@ def rank_program(g, core, T, topo):
         raise ValueError("core %d may not write to core %d" % (core, dst))
     S = T.sem
     V, PE, ACT, SY = g.vector, g.tensor, g.scalar, g.sync
-    mult, add = AluOpType.mult, AluOpType.add
+    mult = AluOpType.mult
     AF = ActivationFunctionType
 
     def cols(t, b, w):
@@ -72,8 +70,9 @@ def rank_program(g, core, T, topo):
     SY.dma_start(T.w2b[:], T.w2[:]).then_inc(S.ld_w2, 16)
 
     V.memset(T.ones[:], 1.0).then_inc(S.c_ones, 1)
-    V.memset(T.cmean[:], 1.0 / (G * 128)).then_inc(S.c_col, 1)
-    V.memset(T.ceps[:], EPS / 128).then_inc(S.c_col, 1)
+    V.memset(T.cmean[:], SC / (G * 128)).then_inc(S.c_col, 1)
+    V.memset(T.ceps[:], EPS * SC / 128).then_inc(S.c_col, 1)
+    V.memset(T.back[:], SC ** 0.5).then_inc(S.c_back, 1)
     g.wait_ge(S.c_ones, 1)
     g.affine_select(T.ident[:], T.ones[:], [[-1, 128]], AluOpType.is_equal, 0.0, 0, 1).then_inc(S.c_id, 1)
 
@@ -110,24 +109,18 @@ def rank_program(g, core, T, topo):
         ACT.wait_ge(S["mm_%d" % b], 1)
         ACT.activation(cols(T.sqb, b, NC), zb, AF.Square).then_inc(S["sq_%d" % b], 1)
         ACT.activation(cols(T.zcb, b, NC), zb, AF.Copy).then_inc(S.e_cp, 1)
-    ACT.wait_ge(S.e_st, 1)
-    ACT.activation(T.rtb[:], T.stp[:, 0:1], AF.Sqrt).then_inc(S.e_rt, 1)
 
-    V.wait_ge(S.e_rt, 1)
-    V.reciprocal(T.y0b[:], T.rtb[:]).then_inc(S.e_rc, 1)
-    V.wait_ge(S.e_rc, 1)
-    V.tensor_scalar(T.nvb[:], T.stp[:, 0:1], T.y0b[:], T.y0b[:], mult, mult).then_inc(S.e_nv, 1)
-    V.wait_ge(S.e_nv, 1)
-    V.tensor_scalar(T.nwb[:], T.nvb[:], -0.5, 1.5, mult, add).then_inc(S.e_nw, 1)
-    V.wait_ge(S.e_nw, 1)
-    V.wait_ge(S.c_id, 1)
-    V.tensor_scalar(T.diag[:], T.ident[:], T.y0b[:], T.nwb[:], mult, mult).then_inc(S.e_diag, 1)
-
+    V.wait_ge(S.e_st, 1)
+    V.reciprocal(T.tb[:], T.stp[:, 0:1]).then_inc(S.e_rc, 1)
+    ACT.wait_ge(S.c_id, 1)
+    ACT.wait_ge(S.e_rc, 1)
+    ACT.activation(T.diag[:], T.ident[:], AF.Sqrt, scale=T.tb[:]).then_inc(S.e_diag, 1)
+    PE.wait_ge(S.c_back, 1)
     PE.wait_ge(S.e_diag, 1)
-    PE.matmul(T.bcp[:, 0:NC], T.ones[:], T.diag[:], True, True).then_inc(S.e_bc, 1)
+    PE.matmul(T.bcp[:, 0:NC], T.back[:], T.diag[:], True, True).then_inc(S.e_bc, 1)
 
-    V.wait_ge(S.e_bc, 1)
     V.wait_ge(S.e_cp, G)
+    V.wait_ge(S.e_bc, 1)
     for b in range(G):
         V.tensor_tensor(T.hb[:, b:TW:4], cols(T.zcb, b, NC), T.bcp[:, 0:NC], mult).then_inc(S.e_h, 1)
     V.wait_ge(S.e_h, G)

@@ -97,11 +97,11 @@ def rank_program(g, core, T, topo):
     PE.wait_ge(S.q_x, 1)
     product(0)
     product(1)
-    mean(0)
     product(2)
+    mean(0)
+    product(3)
     mean(1)
     mean(2)
-    product(3)
     mean(3).then_inc(S.e_st, 1)
 
     for b in range(G):

@@ -1,10 +1,23 @@
-from concourse.mybir import dt, AluOpType, ActivationFunctionType
+import numpy as np
+from concourse.mybir import dt, AluOpType, AxisListType, ActivationFunctionType
 
 NC = 128
 TW = 4 * NC
 G = 4
 EPS = 0.001
-SC = 2.0 ** -44
+
+N1 = 68
+DEG = 13
+NP = DEG + 1
+MID, HALF = 2.5, 1.5
+
+
+def coefficients():
+    i = np.arange(NP)
+    x = np.cos((2 * i + 1) * np.pi / (2 * NP)) * 1.002
+    c = np.linalg.solve(np.vander(x, NP, increasing=True), (MID + HALF * x) ** -0.5)
+    return [float(c[k]) / HALF ** k for k in range(NP)]
+
 
 SCRATCH = {
     "xb": ("sbuf", [128, TW], "bfloat16"),
@@ -24,12 +37,19 @@ SCRATCH = {
     "sqb": ("sbuf", [128, G * NC], "float32"),
     "zcb": ("sbuf", [128, G * NC], "float32"),
     "ones": ("sbuf", [128, 128], "float32"),
-    "back": ("sbuf", [128, 128], "float32"),
     "ident": ("sbuf", [128, 128], "float32"),
-    "diag": ("sbuf", [128, 128], "float32"),
-    "cmean": ("sbuf", [128, 1], "float32"),
-    "ceps": ("sbuf", [128, 1], "float32"),
-    "tb": ("sbuf", [128, 1], "float32"),
+    "cmean": ("sbuf", [128, NP], "float32"),
+    "ceps": ("sbuf", [128, NP], "float32"),
+    "k1": ("sbuf", [128, N1], "float32"),
+    "t1": ("sbuf", [128, N1], "float32"),
+    "fa": ("sbuf", [128, N1 + 1], "float32"),
+    "fb": ("sbuf", [128, N1 + 1], "float32"),
+    "y0b": ("sbuf", [128, 1], "float32"),
+    "w0b": ("sbuf", [128, 1], "float32"),
+    "cv": ("sbuf", [128, NP], "float32"),
+    "eb": ("sbuf", [128, NP + 128], "float32"),
+    "cyb": ("sbuf", [128, NP + 128], "float32"),
+    "sw": ("sbuf", [128, NP + 128], "float32"),
     "yb": ("sbuf", [128, NC], "float32"),
     "zp": ("psum", [128, G * 512], "float32"),
     "stp": ("psum", [128, 512], "float32"),
@@ -38,8 +58,9 @@ SCRATCH = {
 }
 
 SEMAPHORES = (
-    ["ld_x", "ld_w2", "c_ones", "c_col", "c_id", "c_back", "q_x", "q_h", "q_w2a", "q_w2b",
-     "e_cp", "e_st", "e_rc", "e_diag", "e_bc", "e_h", "issued", "sent", "arrived", "e_y", "e_yb", "st_h", "st_y"]
+    ["ld_x", "ld_w2", "c_ones", "c_col", "c_id", "c_k", "c_t", "c_pre", "c_cv", "q_x", "q_h", "q_w2a", "q_w2b",
+     "e_cp", "e_st", "r_1", "r_2", "r_3", "e_sw", "e_bc", "e_h", "issued", "sent", "arrived",
+     "e_y", "e_yb", "st_h", "st_y"]
     + ["ld_w1_%d" % b for b in range(G)]
     + ["q_w1_%d" % b for b in range(G)]
     + ["mm_%d" % b for b in range(G)]
@@ -57,7 +78,7 @@ def rank_program(g, core, T, topo):
         raise ValueError("core %d may not write to core %d" % (core, dst))
     S = T.sem
     V, PE, ACT, SY = g.vector, g.tensor, g.scalar, g.sync
-    mult = AluOpType.mult
+    mult, add, vmax, gt = AluOpType.mult, AluOpType.add, AluOpType.max, AluOpType.is_gt
     AF = ActivationFunctionType
 
     def cols(t, b, w):
@@ -70,11 +91,22 @@ def rank_program(g, core, T, topo):
     SY.dma_start(T.w2b[:], T.w2[:]).then_inc(S.ld_w2, 16)
 
     V.memset(T.ones[:], 1.0).then_inc(S.c_ones, 1)
-    V.memset(T.cmean[:], SC / (G * 128)).then_inc(S.c_col, 1)
-    V.memset(T.ceps[:], EPS * SC / 128).then_inc(S.c_col, 1)
-    V.memset(T.back[:], SC ** 0.5).then_inc(S.c_back, 1)
+    V.memset(T.cmean[:], 1.0 / (G * 128)).then_inc(S.c_col, 1)
+    V.memset(T.ceps[:], EPS / 128).then_inc(S.c_col, 1)
+    V.memset(T.k1[:], 4.0).then_inc(S.c_k, 1)
+    V.memset(T.fa[:, N1:N1 + 1], 2.0 ** 5).then_inc(S.c_pre, 1)
+    V.memset(T.fb[:, N1:N1 + 1], 2.0 ** 10).then_inc(S.c_pre, 1)
+    V.memset(T.eb[:, NP:], 1.0).then_inc(S.c_pre, 1)
+    V.memset(T.cyb[:, NP:], 0.0).then_inc(S.c_pre, 1)
+    V.wait_ge(S.c_ones, 1)
+    V.wait_ge(S.c_k, 1)
+    V.tensor_tensor_scan(T.t1[:], T.k1[:], T.ones[:, 0:N1], 2.0 ** -10, mult, mult).then_inc(S.c_t, 1)
     g.wait_ge(S.c_ones, 1)
     g.affine_select(T.ident[:], T.ones[:], [[-1, 128]], AluOpType.is_equal, 0.0, 0, 1).then_inc(S.c_id, 1)
+    c = coefficients()
+    ACT.wait_ge(S.c_ones, 1)
+    for t in range(NP):
+        ACT.activation(T.cv[:, t:t + 1], T.ones[:, 0:1], AF.Copy, scale=c[DEG - t]).then_inc(S.c_cv, 1)
 
     V.wait_ge(S.ld_x, 16)
     V.quantize_mx(T.xq[:], T.xs[:], T.xb[:]).then_inc(S.q_x, 1)
@@ -89,11 +121,11 @@ def rank_program(g, core, T, topo):
 
     def mean(b):
         PE.wait_ge(S["sq_%d" % b], 1)
-        return PE.matmul(T.stp[:, 0:1], cols(T.sqb, b, NC), T.cmean[:], False, b == G - 1)
+        return PE.matmul(T.stp[:, 0:NP], cols(T.sqb, b, NC), T.cmean[:], False, b == G - 1)
 
     PE.wait_ge(S.c_ones, 1)
     PE.wait_ge(S.c_col, 2)
-    PE.matmul(T.stp[:, 0:1], T.ones[:], T.ceps[:], True, False)
+    PE.matmul(T.stp[:, 0:NP], T.ones[:], T.ceps[:], True, False)
     PE.wait_ge(S.q_x, 1)
     product(0)
     product(1)
@@ -110,14 +142,25 @@ def rank_program(g, core, T, topo):
         ACT.activation(cols(T.sqb, b, NC), zb, AF.Square).then_inc(S["sq_%d" % b], 1)
         ACT.activation(cols(T.zcb, b, NC), zb, AF.Copy).then_inc(S.e_cp, 1)
 
+    a = T.stp[:, 0:1]
+    V.wait_ge(S.c_t, 1)
+    V.wait_ge(S.c_pre, 4)
+    V.wait_ge(S.c_cv, NP)
     V.wait_ge(S.e_st, 1)
-    V.reciprocal(T.tb[:], T.stp[:, 0:1]).then_inc(S.e_rc, 1)
-    ACT.wait_ge(S.c_id, 1)
-    ACT.wait_ge(S.e_rc, 1)
-    ACT.activation(T.diag[:], T.ident[:], AF.Sqrt, scale=T.tb[:]).then_inc(S.e_diag, 1)
-    PE.wait_ge(S.c_back, 1)
-    PE.wait_ge(S.e_diag, 1)
-    PE.matmul(T.bcp[:, 0:NC], T.back[:], T.diag[:], True, True).then_inc(S.e_bc, 1)
+    V.tensor_scalar(T.fb[:, 0:N1], T.t1[:], a, 0.25, gt, vmax).then_inc(S.r_1, 1)
+    V.tensor_scalar(T.fa[:, 0:N1], T.t1[:], a, 0.5, gt, vmax).then_inc(S.r_1, 1)
+    V.wait_ge(S.r_1, 2)
+    V.tensor_reduce(T.w0b[:], T.fb[:], AxisListType.X, mult).then_inc(S.r_2, 1)
+    V.tensor_reduce(T.y0b[:], T.fa[:], AxisListType.X, mult).then_inc(S.r_2, 1)
+    V.wait_ge(S.r_2, 2)
+    V.tensor_scalar(T.eb[:, 0:NP], T.stp[:, 0:NP], T.w0b[:], -MID, mult, add).then_inc(S.r_3, 1)
+    V.tensor_scalar(T.cyb[:, 0:NP], T.cv[:], T.y0b[:], None, mult).then_inc(S.r_3, 1)
+    V.wait_ge(S.r_3, 2)
+    V.tensor_tensor_scan(T.sw[:], T.eb[:], T.cyb[:], 0.0, mult, add).then_inc(S.e_sw, 1)
+
+    PE.wait_ge(S.c_id, 1)
+    PE.wait_ge(S.e_sw, 1)
+    PE.matmul(T.bcp[:, 0:NC], T.sw[:, NP:NP + 128], T.ident[:], True, True).then_inc(S.e_bc, 1)
 
     V.wait_ge(S.e_cp, G)
     V.wait_ge(S.e_bc, 1)

@@ -6,7 +6,7 @@ TW = 4 * NC
 G = 4
 EPS = 0.001
 
-N1 = 68
+N1 = 69
 DEG = 13
 NP = DEG + 1
 MID, HALF = 2.5, 1.5
@@ -16,7 +16,7 @@ def coefficients():
     i = np.arange(NP)
     x = np.cos((2 * i + 1) * np.pi / (2 * NP)) * 1.002
     c = np.linalg.solve(np.vander(x, NP, increasing=True), (MID + HALF * x) ** -0.5)
-    return [float(c[k]) / HALF ** k for k in range(NP)]
+    return [float(c[k]) / HALF ** k * 2.0 ** 0.5 for k in range(NP)]
 
 
 SCRATCH = {
@@ -34,37 +34,40 @@ SCRATCH = {
     "hs": ("sbuf", [128, NC], "uint8"),
     "rq": ("sbuf", [128, NC], "float8_e4m3fn_x4"),
     "rs": ("sbuf", [128, NC], "uint8"),
-    "sqb": ("sbuf", [128, G * NC], "float32"),
-    "zcb": ("sbuf", [128, G * NC], "float32"),
+    "sqj": ("sbuf", [128, G * NC], "float32"),
+    "acc": ("sbuf", [128, 8], "float32"),
     "ones": ("sbuf", [128, 128], "float32"),
     "ident": ("sbuf", [128, 128], "float32"),
-    "cmean": ("sbuf", [128, NP], "float32"),
-    "ceps": ("sbuf", [128, NP], "float32"),
-    "k1": ("sbuf", [128, N1], "float32"),
+    "k4": ("sbuf", [128, N1], "float32"),
+    "kq": ("sbuf", [128, N1], "float32"),
+    "kh": ("sbuf", [128, N1], "float32"),
     "t1": ("sbuf", [128, N1], "float32"),
-    "fa": ("sbuf", [128, N1 + 1], "float32"),
-    "fb": ("sbuf", [128, N1 + 1], "float32"),
-    "y0b": ("sbuf", [128, 1], "float32"),
-    "w0b": ("sbuf", [128, 1], "float32"),
+    "te": ("sbuf", [128, N1], "float32"),
+    "t3": ("sbuf", [128, N1], "float32"),
+    "yt": ("sbuf", [128, N1], "float32"),
+    "dtb": ("sbuf", [128, N1 + NP], "float32"),
+    "mk": ("sbuf", [128, N1 + NP], "float32"),
+    "ee": ("sbuf", [128, N1 + NP], "float32"),
+    "ys": ("sbuf", [128, N1], "float32"),
     "cv": ("sbuf", [128, NP], "float32"),
-    "eb": ("sbuf", [128, NP + 128], "float32"),
-    "cyb": ("sbuf", [128, NP + 128], "float32"),
-    "sw": ("sbuf", [128, NP + 128], "float32"),
+    "pw": ("sbuf", [128, NP], "float32"),
+    "idy": ("sbuf", [128, 128], "bfloat16"),
+    "rt": ("sbuf", [128, G * NC], "bfloat16"),
     "yb": ("sbuf", [128, NC], "float32"),
     "zp": ("psum", [128, G * 512], "float32"),
-    "stp": ("psum", [128, 512], "float32"),
-    "bcp": ("psum", [128, 512], "float32"),
     "yp": ("psum", [128, 512], "float32"),
 }
 
 SEMAPHORES = (
-    ["ld_x", "ld_w2", "c_ones", "c_col", "c_id", "c_k", "c_t", "c_pre", "c_cv", "q_x", "q_h", "q_w2a", "q_w2b",
-     "e_cp", "e_st", "r_1", "r_2", "r_3", "e_sw", "e_bc", "e_h", "issued", "sent", "arrived",
+    ["ld_x", "ld_w2", "c_ones", "c_id", "c_k", "c_t", "c_pre", "c_cv", "q_x", "q_h", "q_w2a", "q_w2b",
+     "e_t3", "r_1", "r_2", "r_3", "e_idy", "e_h", "issued", "sent", "arrived",
      "e_y", "e_yb", "st_h", "st_y"]
     + ["ld_w1_%d" % b for b in range(G)]
     + ["q_w1_%d" % b for b in range(G)]
     + ["mm_%d" % b for b in range(G)]
     + ["sq_%d" % b for b in range(G)]
+    + ["sc_%d" % b for b in range(G)]
+    + ["tr_%d" % b for b in range(G)]
 )
 
 
@@ -78,11 +81,14 @@ def rank_program(g, core, T, topo):
         raise ValueError("core %d may not write to core %d" % (core, dst))
     S = T.sem
     V, PE, ACT, SY = g.vector, g.tensor, g.scalar, g.sync
-    mult, add, vmax, gt = AluOpType.mult, AluOpType.add, AluOpType.max, AluOpType.is_gt
+    mult, add, sub, vmax, gt = AluOpType.mult, AluOpType.add, AluOpType.subtract, AluOpType.max, AluOpType.is_gt
     AF = ActivationFunctionType
 
     def cols(t, b, w):
         return t[:, b * w:(b + 1) * w]
+
+    def bank(b):
+        return T.zp[:, 512 * b:512 * b + NC]
 
     SY.dma_start(T.xb[:], T.x[:]).then_inc(S.ld_x, 16)
     for b in range(G):
@@ -91,16 +97,21 @@ def rank_program(g, core, T, topo):
     SY.dma_start(T.w2b[:], T.w2[:]).then_inc(S.ld_w2, 16)
 
     V.memset(T.ones[:], 1.0).then_inc(S.c_ones, 1)
-    V.memset(T.cmean[:], 1.0 / (G * 128)).then_inc(S.c_col, 1)
-    V.memset(T.ceps[:], EPS / 128).then_inc(S.c_col, 1)
-    V.memset(T.k1[:], 4.0).then_inc(S.c_k, 1)
-    V.memset(T.fa[:, N1:N1 + 1], 2.0 ** 5).then_inc(S.c_pre, 1)
-    V.memset(T.fb[:, N1:N1 + 1], 2.0 ** 10).then_inc(S.c_pre, 1)
-    V.memset(T.eb[:, NP:], 1.0).then_inc(S.c_pre, 1)
-    V.memset(T.cyb[:, NP:], 0.0).then_inc(S.c_pre, 1)
+    V.memset(T.k4[:], 4.0).then_inc(S.c_k, 1)
+    V.memset(T.kq[:], 0.25).then_inc(S.c_k, 1)
+    V.memset(T.kh[:], 0.5).then_inc(S.c_k, 1)
+    V.memset(T.dtb[:, N1:N1 + 1], -MID).then_inc(S.c_pre, 1)
+    V.memset(T.dtb[:, N1 + 1:], 0.0).then_inc(S.c_pre, 1)
+    V.memset(T.mk[:, N1 + 1:], 1.0).then_inc(S.c_pre, 1)
+    V.memset(T.acc[:, 4:5], 2 * EPS).then_inc(S.c_pre, 1)
     V.wait_ge(S.c_ones, 1)
-    V.wait_ge(S.c_k, 1)
-    V.tensor_tensor_scan(T.t1[:], T.k1[:], T.ones[:, 0:N1], 2.0 ** -10, mult, mult).then_inc(S.c_t, 1)
+    V.wait_ge(S.c_k, 3)
+    V.tensor_tensor_scan(T.t1[:], T.k4[:], T.ones[:, 0:N1], 2.0 ** -12, mult, mult).then_inc(S.c_t, 1)
+    V.tensor_tensor_scan(T.dtb[:, 0:N1], T.kq[:], T.ones[:, 0:N1], 0.75 * 2.0 ** 12, mult, mult).then_inc(S.c_t, 1)
+    V.tensor_tensor_scan(T.yt[:], T.kh[:], T.ones[:, 0:N1], 2.0 ** 6, mult, mult).then_inc(S.c_t, 1)
+    V.wait_ge(S.c_t, 3)
+    V.tensor_scalar(T.te[:], T.t1[:], -2 * EPS, None, add).then_inc(S.c_pre, 1)
+    V.memset(T.dtb[:, N1 - 1:N1], 2.0 ** -126).then_inc(S.c_pre, 1)
     g.wait_ge(S.c_ones, 1)
     g.affine_select(T.ident[:], T.ones[:], [[-1, 128]], AluOpType.is_equal, 0.0, 0, 1).then_inc(S.c_id, 1)
     c = coefficients()
@@ -114,58 +125,57 @@ def rank_program(g, core, T, topo):
         V.wait_ge(S["ld_w1_%d" % b], 16)
         V.quantize_mx(cols(T.w1q, b, NC), cols(T.w1s, b, NC), cols(T.w1b, b, TW)).then_inc(S["q_w1_%d" % b], 1)
 
-    def product(b):
-        PE.wait_ge(S["q_w1_%d" % b], 1)
-        PE.matmul_mx(T.zp[:, 512 * b:512 * b + NC], cols(T.w1q, b, NC), cols(T.w1s, b, NC),
-                     T.xq[:], T.xs[:], True, True).then_inc(S["mm_%d" % b], 1)
-
-    def mean(b):
-        PE.wait_ge(S["sq_%d" % b], 1)
-        return PE.matmul(T.stp[:, 0:NP], cols(T.sqb, b, NC), T.cmean[:], False, b == G - 1)
-
-    PE.wait_ge(S.c_ones, 1)
-    PE.wait_ge(S.c_col, 2)
-    PE.matmul(T.stp[:, 0:NP], T.ones[:], T.ceps[:], True, False)
     PE.wait_ge(S.q_x, 1)
-    product(0)
-    product(1)
-    product(2)
-    mean(0)
-    product(3)
-    mean(1)
-    mean(2)
-    mean(3).then_inc(S.e_st, 1)
+    for b in range(G):
+        PE.wait_ge(S["q_w1_%d" % b], 1)
+        PE.matmul_mx(bank(b), T.xq[:], T.xs[:], cols(T.w1q, b, NC), cols(T.w1s, b, NC),
+                     True, True).then_inc(S["mm_%d" % b], 1)
 
     for b in range(G):
-        zb = T.zp[:, 512 * b:512 * b + NC]
         ACT.wait_ge(S["mm_%d" % b], 1)
-        ACT.activation(cols(T.sqb, b, NC), zb, AF.Square).then_inc(S["sq_%d" % b], 1)
-        ACT.activation(cols(T.zcb, b, NC), zb, AF.Copy).then_inc(S.e_cp, 1)
+        ACT.activation(cols(T.sqj, b, NC), bank(b), AF.Square, scale=2.0 ** -4,
+                       accum_out=T.acc[:, b:b + 1]).then_inc(S["sq_%d" % b], 1)
 
-    a = T.stp[:, 0:1]
-    V.wait_ge(S.c_t, 1)
-    V.wait_ge(S.c_pre, 4)
+    V.wait_ge(S.c_pre, 6)
     V.wait_ge(S.c_cv, NP)
-    V.wait_ge(S.e_st, 1)
-    V.tensor_scalar(T.fb[:, 0:N1], T.t1[:], a, 0.25, gt, vmax).then_inc(S.r_1, 1)
-    V.tensor_scalar(T.fa[:, 0:N1], T.t1[:], a, 0.5, gt, vmax).then_inc(S.r_1, 1)
+    V.wait_ge(S.sq_0, 1)
+    V.wait_ge(S.sq_1, 1)
+    V.tensor_scalar(T.t3[:], T.te[:], T.acc[:, 0:1], T.acc[:, 1:2], sub, sub).then_inc(S.e_t3, 1)
+    V.wait_ge(S.e_t3, 1)
+    V.wait_ge(S.sq_2, 1)
+    V.wait_ge(S.sq_3, 1)
+    V.tensor_scalar(T.mk[:, 0:N1], T.t3[:], T.acc[:, 2:3], T.acc[:, 3:4], sub, gt).then_inc(S.r_1, 1)
+    V.tensor_reduce(T.mk[:, N1:N1 + 1], T.acc[:, 0:5], AxisListType.X, add).then_inc(S.r_1, 1)
     V.wait_ge(S.r_1, 2)
-    V.tensor_reduce(T.w0b[:], T.fb[:], AxisListType.X, mult).then_inc(S.r_2, 1)
-    V.tensor_reduce(T.y0b[:], T.fa[:], AxisListType.X, mult).then_inc(S.r_2, 1)
+    V.tensor_tensor_scan(T.ee[:], T.mk[:], T.dtb[:], 0.0, mult, add).then_inc(S.r_2, 1)
+    V.tensor_tensor_scan(T.ys[:], T.mk[:, 0:N1], T.yt[:], 0.0, mult, vmax).then_inc(S.r_2, 1)
     V.wait_ge(S.r_2, 2)
-    V.tensor_scalar(T.eb[:, 0:NP], T.stp[:, 0:NP], T.w0b[:], -MID, mult, add).then_inc(S.r_3, 1)
-    V.tensor_scalar(T.cyb[:, 0:NP], T.cv[:], T.y0b[:], None, mult).then_inc(S.r_3, 1)
-    V.wait_ge(S.r_3, 2)
-    V.tensor_tensor_scan(T.sw[:], T.eb[:], T.cyb[:], 0.0, mult, add).then_inc(S.e_sw, 1)
+    V.tensor_tensor_scan(T.pw[:], T.ee[:, N1:N1 + NP], T.cv[:], 0.0, mult, add).then_inc(S.r_3, 1)
+    p_col = T.pw[:, NP - 1:NP]
 
-    PE.wait_ge(S.c_id, 1)
-    PE.wait_ge(S.e_sw, 1)
-    PE.matmul(T.bcp[:, 0:NC], T.sw[:, NP:NP + 128], T.ident[:], True, True).then_inc(S.e_bc, 1)
+    ACT.wait_ge(S.c_id, 1)
+    ACT.wait_ge(S.r_2, 2)
+    ACT.activation(T.idy[:], T.ident[:], AF.Identity, scale=T.ys[:, N1 - 1:N1]).then_inc(S.e_idy, 1)
 
-    V.wait_ge(S.e_cp, G)
-    V.wait_ge(S.e_bc, 1)
-    for b in range(G):
-        V.tensor_tensor(T.hb[:, b:TW:4], cols(T.zcb, b, NC), T.bcp[:, 0:NC], mult).then_inc(S.e_h, 1)
+    V.wait_ge(S.r_3, 1)
+    for b in (0, 1):
+        V.tensor_scalar(cols(T.rt, b, NC), bank(b), p_col, None, mult).then_inc(S["sc_%d" % b], 1)
+    ACT.wait_ge(S.r_3, 1)
+    for b in (2, 3):
+        ACT.activation(cols(T.rt, b, NC), bank(b), AF.Identity, scale=p_col).then_inc(S["sc_%d" % b], 1)
+
+    PE.wait_ge(S.e_idy, 1)
+    for b in (0, 2, 1, 3):
+        PE.wait_ge(S["sc_%d" % b], 1)
+        PE.matmul(bank(b), cols(T.rt, b, NC), T.idy[:], True, True).then_inc(S["tr_%d" % b], 1)
+
+    for b in (0, 1):
+        V.wait_ge(S["tr_%d" % b], 1)
+        V.tensor_copy(T.hb[:, b:TW:4], bank(b)).then_inc(S.e_h, 1)
+    for b in (2, 3):
+        ACT.wait_ge(S["tr_%d" % b], 1)
+        ACT.activation(T.hb[:, b:TW:4], bank(b), AF.Copy).then_inc(S.e_h, 1)
+
     V.wait_ge(S.e_h, G)
     V.quantize_mx(T.hq[:], T.hs[:], T.hb[:]).then_inc(S.q_h, 1)
     V.wait_ge(S.ld_w2, 16)

@@ -1,23 +1,13 @@
-import numpy as np
 from concourse.mybir import dt, AluOpType, AxisListType, ActivationFunctionType
 
 NC = 128
 TW = 4 * NC
 G = 4
 EPS = 0.001
+HC = NC // 2
 
-N1 = 69
-DEG = 13
-NP = DEG + 1
-MID, HALF = 2.5, 1.5
-
-
-def coefficients():
-    i = np.arange(NP)
-    x = np.cos((2 * i + 1) * np.pi / (2 * NP)) * 1.002
-    c = np.linalg.solve(np.vander(x, NP, increasing=True), (MID + HALF * x) ** -0.5)
-    return [float(c[k]) / HALF ** k * 2.0 ** 0.5 for k in range(NP)]
-
+C = 2.0 ** -40
+SQ = (C / (G * 128)) ** 0.5
 
 SCRATCH = {
     "xb": ("sbuf", [128, TW], "bfloat16"),
@@ -35,40 +25,40 @@ SCRATCH = {
     "rq": ("sbuf", [128, NC], "float8_e4m3fn_x4"),
     "rs": ("sbuf", [128, NC], "uint8"),
     "sqj": ("sbuf", [128, G * NC], "float32"),
-    "acc": ("sbuf", [128, 8], "float32"),
+    "acc": ("sbuf", [128, 4], "float32"),
+    "acl": ("sbuf", [128, 1], "float32"),
+    "pre": ("sbuf", [128, 1], "float32"),
+    "rr": ("sbuf", [128, 1], "float32"),
+    "ri": ("sbuf", [128, 1], "float32"),
+    "cc": ("sbuf", [128, 1], "float32"),
+    "sc": ("sbuf", [128, 1], "float32"),
+    "z0": ("sbuf", [128, NC], "float32"),
     "ones": ("sbuf", [128, 128], "float32"),
     "ident": ("sbuf", [128, 128], "float32"),
-    "k4": ("sbuf", [128, N1], "float32"),
-    "kq": ("sbuf", [128, N1], "float32"),
-    "kh": ("sbuf", [128, N1], "float32"),
-    "t1": ("sbuf", [128, N1], "float32"),
-    "te": ("sbuf", [128, N1], "float32"),
-    "t3": ("sbuf", [128, N1], "float32"),
-    "yt": ("sbuf", [128, N1], "float32"),
-    "dtb": ("sbuf", [128, N1 + NP], "float32"),
-    "mk": ("sbuf", [128, N1 + NP], "float32"),
-    "ee": ("sbuf", [128, N1 + NP], "float32"),
-    "ys": ("sbuf", [128, N1], "float32"),
-    "cv": ("sbuf", [128, NP], "float32"),
-    "pw": ("sbuf", [128, NP], "float32"),
     "idy": ("sbuf", [128, 128], "bfloat16"),
     "rt": ("sbuf", [128, G * NC], "bfloat16"),
     "yb": ("sbuf", [128, NC], "float32"),
     "zp": ("psum", [128, G * 512], "float32"),
+    "tp": ("psum", [128, 512], "float32"),
     "yp": ("psum", [128, 512], "float32"),
 }
 
 SEMAPHORES = (
-    ["ld_x", "ld_w2", "c_ones", "c_id", "c_k", "c_t", "c_pre", "c_cv", "q_x", "q_h", "q_w2a", "q_w2b",
-     "e_t3", "r_1", "r_2", "r_3", "e_idy", "e_h", "issued", "sent", "arrived",
+    ["ld_x", "ld_w2", "c_ones", "c_id", "c_eps", "c_c", "e_sc", "e_z0", "q_x", "q_h", "q_w2a", "q_w2b",
+     "e_pre", "r_1", "r_2", "e_idy", "e_h", "tr_3a", "tr_3b", "issued", "sent", "arrived",
      "e_y", "e_yb", "st_h", "st_y"]
     + ["ld_w1_%d" % b for b in range(G)]
     + ["q_w1_%d" % b for b in range(G)]
     + ["mm_%d" % b for b in range(G)]
     + ["sq_%d" % b for b in range(G)]
     + ["sc_%d" % b for b in range(G)]
-    + ["tr_%d" % b for b in range(G)]
+    + ["tr_%d" % b for b in range(G - 1)]
 )
+
+
+def halves(mask):
+    bits = [e for e in range(mask.bit_length()) if mask >> e & 1]
+    return sum(1 << e for e in bits[0::2]), sum(1 << e for e in bits[1::2])
 
 
 def rank_program(g, core, T, topo):
@@ -81,8 +71,9 @@ def rank_program(g, core, T, topo):
         raise ValueError("core %d may not write to core %d" % (core, dst))
     S = T.sem
     V, PE, ACT, SY = g.vector, g.tensor, g.scalar, g.sync
-    mult, add, sub, vmax, gt = AluOpType.mult, AluOpType.add, AluOpType.subtract, AluOpType.max, AluOpType.is_gt
+    mult, add = AluOpType.mult, AluOpType.add
     AF = ActivationFunctionType
+    L = G - 1
 
     def cols(t, b, w):
         return t[:, b * w:(b + 1) * w]
@@ -96,28 +87,16 @@ def rank_program(g, core, T, topo):
         q.dma_start(cols(T.w1b, b, TW), cols(T.w1, b, TW)).then_inc(S["ld_w1_%d" % b], 16)
     SY.dma_start(T.w2b[:], T.w2[:]).then_inc(S.ld_w2, 16)
 
+    V.memset(T.cc[:], C).then_inc(S.c_c, 1)
     V.memset(T.ones[:], 1.0).then_inc(S.c_ones, 1)
-    V.memset(T.k4[:], 4.0).then_inc(S.c_k, 1)
-    V.memset(T.kq[:], 0.25).then_inc(S.c_k, 1)
-    V.memset(T.kh[:], 0.5).then_inc(S.c_k, 1)
-    V.memset(T.dtb[:, N1:N1 + 1], -MID).then_inc(S.c_pre, 1)
-    V.memset(T.dtb[:, N1 + 1:], 0.0).then_inc(S.c_pre, 1)
-    V.memset(T.mk[:, N1 + 1:], 1.0).then_inc(S.c_pre, 1)
-    V.memset(T.acc[:, 4:5], 2 * EPS).then_inc(S.c_pre, 1)
-    V.wait_ge(S.c_ones, 1)
-    V.wait_ge(S.c_k, 3)
-    V.tensor_tensor_scan(T.t1[:], T.k4[:], T.ones[:, 0:N1], 2.0 ** -12, mult, mult).then_inc(S.c_t, 1)
-    V.tensor_tensor_scan(T.dtb[:, 0:N1], T.kq[:], T.ones[:, 0:N1], 0.75 * 2.0 ** 12, mult, mult).then_inc(S.c_t, 1)
-    V.tensor_tensor_scan(T.yt[:], T.kh[:], T.ones[:, 0:N1], 2.0 ** 6, mult, mult).then_inc(S.c_t, 1)
-    V.wait_ge(S.c_t, 3)
-    V.tensor_scalar(T.te[:], T.t1[:], -2 * EPS, None, add).then_inc(S.c_pre, 1)
-    V.memset(T.dtb[:, N1 - 1:N1], 2.0 ** -126).then_inc(S.c_pre, 1)
+    V.memset(T.acc[:, 3:4], C * EPS).then_inc(S.c_eps, 1)
     g.wait_ge(S.c_ones, 1)
     g.affine_select(T.ident[:], T.ones[:], [[-1, 128]], AluOpType.is_equal, 0.0, 0, 1).then_inc(S.c_id, 1)
-    c = coefficients()
-    ACT.wait_ge(S.c_ones, 1)
-    for t in range(NP):
-        ACT.activation(T.cv[:, t:t + 1], T.ones[:, 0:1], AF.Copy, scale=c[DEG - t]).then_inc(S.c_cv, 1)
+    ACT.wait_ge(S.c_c, 1)
+    ACT.activation(T.sc[:], T.cc[:], AF.Sqrt).then_inc(S.e_sc, 1)
+    ACT.wait_ge(S.e_sc, 1)
+    ACT.wait_ge(S.c_id, 1)
+    ACT.activation(T.idy[:], T.ident[:], AF.Identity, scale=T.sc[:]).then_inc(S.e_idy, 1)
 
     V.wait_ge(S.ld_x, 16)
     V.quantize_mx(T.xq[:], T.xs[:], T.xb[:]).then_inc(S.q_x, 1)
@@ -133,50 +112,54 @@ def rank_program(g, core, T, topo):
 
     for b in range(G):
         ACT.wait_ge(S["mm_%d" % b], 1)
-        ACT.activation(cols(T.sqj, b, NC), bank(b), AF.Square, scale=2.0 ** -4,
-                       accum_out=T.acc[:, b:b + 1]).then_inc(S["sq_%d" % b], 1)
+        ACT.activation(cols(T.sqj, b, NC), bank(b), AF.Square, scale=SQ,
+                       accum_out=(T.acc[:, b:b + 1] if b < L else T.acl[:])).then_inc(S["sq_%d" % b], 1)
 
-    V.wait_ge(S.c_pre, 6)
-    V.wait_ge(S.c_cv, NP)
-    V.wait_ge(S.sq_0, 1)
-    V.wait_ge(S.sq_1, 1)
-    V.tensor_scalar(T.t3[:], T.te[:], T.acc[:, 0:1], T.acc[:, 1:2], sub, sub).then_inc(S.e_t3, 1)
-    V.wait_ge(S.e_t3, 1)
-    V.wait_ge(S.sq_2, 1)
-    V.wait_ge(S.sq_3, 1)
-    V.tensor_scalar(T.mk[:, 0:N1], T.t3[:], T.acc[:, 2:3], T.acc[:, 3:4], sub, gt).then_inc(S.r_1, 1)
-    V.tensor_reduce(T.mk[:, N1:N1 + 1], T.acc[:, 0:5], AxisListType.X, add).then_inc(S.r_1, 1)
-    V.wait_ge(S.r_1, 2)
-    V.tensor_tensor_scan(T.ee[:], T.mk[:], T.dtb[:], 0.0, mult, add).then_inc(S.r_2, 1)
-    V.tensor_tensor_scan(T.ys[:], T.mk[:, 0:N1], T.yt[:], 0.0, mult, vmax).then_inc(S.r_2, 1)
-    V.wait_ge(S.r_2, 2)
-    V.tensor_tensor_scan(T.pw[:], T.ee[:, N1:N1 + NP], T.cv[:], 0.0, mult, add).then_inc(S.r_3, 1)
-    p_col = T.pw[:, NP - 1:NP]
+    V.wait_ge(S.c_eps, 1)
+    for b in range(L):
+        V.wait_ge(S["sq_%d" % b], 1)
+    V.tensor_reduce(T.pre[:], T.acc[:], AxisListType.X, add).then_inc(S.e_pre, 1)
+    V.tensor_copy(T.z0[:], bank(0)).then_inc(S.e_z0, 1)
 
-    ACT.wait_ge(S.c_id, 1)
-    ACT.wait_ge(S.r_2, 2)
-    ACT.activation(T.idy[:], T.ident[:], AF.Identity, scale=T.ys[:, N1 - 1:N1]).then_inc(S.e_idy, 1)
+    ACT.wait_ge(S["sq_%d" % L], 1)
+    ACT.wait_ge(S.e_pre, 1)
+    ACT.activation(T.rr[:], T.acl[:], AF.Sqrt, bias=T.pre[:]).then_inc(S.r_1, 1)
+    V.wait_ge(S.r_1, 1)
+    V.reciprocal(T.ri[:], T.rr[:]).then_inc(S.r_2, 1)
 
-    V.wait_ge(S.r_3, 1)
-    for b in (0, 1):
-        V.tensor_scalar(cols(T.rt, b, NC), bank(b), p_col, None, mult).then_inc(S["sc_%d" % b], 1)
-    ACT.wait_ge(S.r_3, 1)
-    for b in (2, 3):
-        ACT.activation(cols(T.rt, b, NC), bank(b), AF.Identity, scale=p_col).then_inc(S["sc_%d" % b], 1)
+    V.wait_ge(S.r_2, 1)
+    V.wait_ge(S.e_z0, 1)
+    V.tensor_scalar(T.rt[:, 0:HC], T.z0[:, 0:HC], T.ri[:], None, mult).then_inc(S.sc_0, 1)
+    for b in (1, 3):
+        V.tensor_scalar(cols(T.rt, b, NC), bank(b), T.ri[:], None, mult).then_inc(S["sc_%d" % b], 1)
+    ACT.wait_ge(S.r_2, 1)
+    ACT.wait_ge(S.e_z0, 1)
+    ACT.activation(T.rt[:, HC:NC], T.z0[:, HC:NC], AF.Identity, scale=T.ri[:]).then_inc(S.sc_0, 1)
+    ACT.activation(cols(T.rt, 2, NC), bank(2), AF.Identity, scale=T.ri[:]).then_inc(S.sc_2, 1)
 
     PE.wait_ge(S.e_idy, 1)
-    for b in (0, 2, 1, 3):
+    PE.wait_ge(S.e_z0, 1)
+    PE.wait_ge(S.sc_0, 2)
+    PE.matmul(bank(0), cols(T.rt, 0, NC), T.idy[:], True, True).then_inc(S.tr_0, 1)
+    for b in (1, 2):
         PE.wait_ge(S["sc_%d" % b], 1)
         PE.matmul(bank(b), cols(T.rt, b, NC), T.idy[:], True, True).then_inc(S["tr_%d" % b], 1)
+    PE.wait_ge(S["sc_%d" % L], 1)
+    PE.matmul(T.zp[:, 512 * L:512 * L + HC], cols(T.rt, L, NC), T.idy[:, 0:HC], True, True).then_inc(S.tr_3a, 1)
+    PE.matmul(T.tp[:, 0:HC], cols(T.rt, L, NC), T.idy[:, HC:NC], True, True).then_inc(S.tr_3b, 1)
 
     for b in (0, 1):
-        V.wait_ge(S["tr_%d" % b], 1)
-        V.tensor_copy(T.hb[:, b:TW:4], bank(b)).then_inc(S.e_h, 1)
-    for b in (2, 3):
         ACT.wait_ge(S["tr_%d" % b], 1)
         ACT.activation(T.hb[:, b:TW:4], bank(b), AF.Copy).then_inc(S.e_h, 1)
+    ACT.wait_ge(S.tr_3a, 1)
+    ACT.activation(T.hb[:, L:4 * HC:4], T.zp[:, 512 * L:512 * L + HC], AF.Copy).then_inc(S.e_h, 1)
+    V.wait_ge(S.tr_2, 1)
+    V.tensor_copy(T.hb[:, 2:TW:4], bank(2)).then_inc(S.e_h, 1)
+    V.wait_ge(S.tr_3b, 1)
+    V.tensor_copy(T.hb[:, 4 * HC + L:TW:4], T.tp[:, 0:HC]).then_inc(S.e_h, 1)
+    parts = G + 1
 
-    V.wait_ge(S.e_h, G)
+    V.wait_ge(S.e_h, parts)
     V.quantize_mx(T.hq[:], T.hs[:], T.hb[:]).then_inc(S.q_h, 1)
     V.wait_ge(S.ld_w2, 16)
     V.quantize_mx(cols(T.w2q, 0, NC), cols(T.w2s, 0, NC), cols(T.w2b, 0, TW)).then_inc(S.q_w2a, 1)
@@ -184,14 +167,14 @@ def rank_program(g, core, T, topo):
 
     rid, pid, _ = topo.addr(dst)
     mask = topo.mask(core, dst)
-    engines = bin(mask).count("1")
+    m_codes, m_plane = halves(mask)
     g.wait_ge(S.q_h, 1)
-    g.remote_dma(T.rq[:].bitcast(dt.uint8), T.hq[:].bitcast(dt.uint8), S.arrived, S.sent, pid, rid, mask)
-    g.remote_dma(T.rs[:], T.hs[:], S.arrived, S.sent, pid, rid, mask)
+    g.remote_dma(T.rq[:].bitcast(dt.uint8), T.hq[:].bitcast(dt.uint8), S.arrived, S.sent, pid, rid, m_codes)
+    g.remote_dma(T.rs[:], T.hs[:], S.arrived, S.sent, pid, rid, m_plane)
     g.sem_inc(S.issued, 1)
-    g.wait_ge(S.sent, 2 * engines)
+    g.wait_ge(S.sent, bin(mask).count("1"))
 
-    SY.wait_ge(S.e_h, G)
+    SY.wait_ge(S.e_h, parts)
     SY.wait_ge(S.issued, 1)
     SY.dma_start(T.h[:], T.hb[:]).then_inc(S.st_h, 16)
 
@@ -200,7 +183,7 @@ def rank_program(g, core, T, topo):
     PE.matmul_mx(T.yp[:, 0:NC], cols(T.w2q, 0, NC), cols(T.w2s, 0, NC), T.hq[:], T.hs[:], True, False)
     PE.wait_ge(S.q_w2b, 1)
     src = T.cores[(rank + 1) % n]
-    PE.wait_ge(S.arrived, 2 * bin(topo.mask(src, core)).count("1"))
+    PE.wait_ge(S.arrived, bin(topo.mask(src, core)).count("1"))
     PE.matmul_mx(T.yp[:, 0:NC], cols(T.w2q, 1, NC), cols(T.w2s, 1, NC), T.rq[:], T.rs[:], False, True).then_inc(S.e_y, 1)
 
     V.wait_ge(S.e_y, 1)

from concourse.mybir import dt, AluOpType, AxisListType, ActivationFunctionType

NC = 128
TW = 4 * NC
G = 4
EPS = 0.001
HC = NC // 2

C = 2.0 ** -40
SQ = (C / (G * 128)) ** 0.5

SCRATCH = {
    "xb": ("sbuf", [128, TW], "bfloat16"),
    "w1b": ("sbuf", [128, G * TW], "bfloat16"),
    "w2b": ("sbuf", [128, 2 * TW], "bfloat16"),
    "xq": ("sbuf", [128, NC], "float8_e4m3fn_x4"),
    "xs": ("sbuf", [128, NC], "uint8"),
    "w1q": ("sbuf", [128, G * NC], "float8_e4m3fn_x4"),
    "w1s": ("sbuf", [128, G * NC], "uint8"),
    "w2q": ("sbuf", [128, 2 * NC], "float8_e4m3fn_x4"),
    "w2s": ("sbuf", [128, 2 * NC], "uint8"),
    "hb": ("sbuf", [128, TW], "bfloat16"),
    "hq": ("sbuf", [128, NC], "float8_e4m3fn_x4"),
    "hs": ("sbuf", [128, NC], "uint8"),
    "rq": ("sbuf", [128, NC], "float8_e4m3fn_x4"),
    "rs": ("sbuf", [128, NC], "uint8"),
    "sqj": ("sbuf", [128, G * NC], "float32"),
    "acc": ("sbuf", [128, 4], "float32"),
    "acl": ("sbuf", [128, 1], "float32"),
    "pre": ("sbuf", [128, 1], "float32"),
    "rr": ("sbuf", [128, 1], "float32"),
    "ri": ("sbuf", [128, 1], "float32"),
    "cc": ("sbuf", [128, 1], "float32"),
    "sc": ("sbuf", [128, 1], "float32"),
    "z0": ("sbuf", [128, NC], "float32"),
    "ones": ("sbuf", [128, 128], "float32"),
    "ident": ("sbuf", [128, 128], "float32"),
    "idy": ("sbuf", [128, 128], "bfloat16"),
    "rt": ("sbuf", [128, G * NC], "bfloat16"),
    "yb": ("sbuf", [128, NC], "float32"),
    "zp": ("psum", [128, G * 512], "float32"),
    "tp": ("psum", [128, 512], "float32"),
    "yp": ("psum", [128, 512], "float32"),
}

SEMAPHORES = (
    ["ld_x", "ld_w2", "c_ones", "c_id", "c_eps", "c_c", "e_sc", "e_z0", "q_x", "q_h", "q_w2a", "q_w2b",
     "e_pre", "r_1", "r_2", "e_idy", "e_h", "tr_3a", "tr_3b", "issued", "sent", "arrived",
     "e_y", "e_yb", "st_h", "st_y"]
    + ["ld_w1_%d" % b for b in range(G)]
    + ["q_w1_%d" % b for b in range(G)]
    + ["mm_%d" % b for b in range(G)]
    + ["sq_%d" % b for b in range(G)]
    + ["sc_%d" % b for b in range(G)]
    + ["tr_%d" % b for b in range(G - 1)]
)


def halves(mask):
    bits = [e for e in range(mask.bit_length()) if mask >> e & 1]
    return sum(1 << e for e in bits[0::2]), sum(1 << e for e in bits[1::2])


def rank_program(g, core, T, topo):
    rank = T.rank_of(core)
    if rank is None:
        return
    n = len(T.cores)
    dst = T.cores[(rank - 1) % n]
    if not topo.may_write(core, dst):
        raise ValueError("core %d may not write to core %d" % (core, dst))
    S = T.sem
    V, PE, ACT, SY = g.vector, g.tensor, g.scalar, g.sync
    mult, add = AluOpType.mult, AluOpType.add
    AF = ActivationFunctionType
    L = G - 1

    def cols(t, b, w):
        return t[:, b * w:(b + 1) * w]

    def bank(b):
        return T.zp[:, 512 * b:512 * b + NC]

    SY.dma_start(T.xb[:], T.x[:]).then_inc(S.ld_x, 16)
    for b in range(G):
        q = ACT if b % 2 == 0 else SY
        q.dma_start(cols(T.w1b, b, TW), cols(T.w1, b, TW)).then_inc(S["ld_w1_%d" % b], 16)
    SY.dma_start(T.w2b[:], T.w2[:]).then_inc(S.ld_w2, 16)

    V.memset(T.cc[:], C).then_inc(S.c_c, 1)
    V.memset(T.ones[:], 1.0).then_inc(S.c_ones, 1)
    V.memset(T.acc[:, 3:4], C * EPS).then_inc(S.c_eps, 1)
    g.wait_ge(S.c_ones, 1)
    g.affine_select(T.ident[:], T.ones[:], [[-1, 128]], AluOpType.is_equal, 0.0, 0, 1).then_inc(S.c_id, 1)
    ACT.wait_ge(S.c_c, 1)
    ACT.activation(T.sc[:], T.cc[:], AF.Sqrt).then_inc(S.e_sc, 1)
    ACT.wait_ge(S.e_sc, 1)
    ACT.wait_ge(S.c_id, 1)
    ACT.activation(T.idy[:], T.ident[:], AF.Identity, scale=T.sc[:]).then_inc(S.e_idy, 1)

    V.wait_ge(S.ld_x, 16)
    V.quantize_mx(T.xq[:], T.xs[:], T.xb[:]).then_inc(S.q_x, 1)
    for b in range(G):
        V.wait_ge(S["ld_w1_%d" % b], 16)
        V.quantize_mx(cols(T.w1q, b, NC), cols(T.w1s, b, NC), cols(T.w1b, b, TW)).then_inc(S["q_w1_%d" % b], 1)

    PE.wait_ge(S.q_x, 1)
    for b in range(G):
        PE.wait_ge(S["q_w1_%d" % b], 1)
        PE.matmul_mx(bank(b), T.xq[:], T.xs[:], cols(T.w1q, b, NC), cols(T.w1s, b, NC),
                     True, True).then_inc(S["mm_%d" % b], 1)

    for b in range(G):
        ACT.wait_ge(S["mm_%d" % b], 1)
        ACT.activation(cols(T.sqj, b, NC), bank(b), AF.Square, scale=SQ,
                       accum_out=(T.acc[:, b:b + 1] if b < L else T.acl[:])).then_inc(S["sq_%d" % b], 1)

    V.wait_ge(S.c_eps, 1)
    for b in range(L):
        V.wait_ge(S["sq_%d" % b], 1)
    V.tensor_reduce(T.pre[:], T.acc[:], AxisListType.X, add).then_inc(S.e_pre, 1)
    V.tensor_copy(T.z0[:], bank(0)).then_inc(S.e_z0, 1)

    ACT.wait_ge(S["sq_%d" % L], 1)
    ACT.wait_ge(S.e_pre, 1)
    ACT.activation(T.rr[:], T.acl[:], AF.Sqrt, bias=T.pre[:]).then_inc(S.r_1, 1)
    V.wait_ge(S.r_1, 1)
    V.reciprocal(T.ri[:], T.rr[:]).then_inc(S.r_2, 1)

    V.wait_ge(S.r_2, 1)
    V.wait_ge(S.e_z0, 1)
    V.tensor_scalar(T.rt[:, 0:HC], T.z0[:, 0:HC], T.ri[:], None, mult).then_inc(S.sc_0, 1)
    for b in (1, 3):
        V.tensor_scalar(cols(T.rt, b, NC), bank(b), T.ri[:], None, mult).then_inc(S["sc_%d" % b], 1)
    ACT.wait_ge(S.r_2, 1)
    ACT.wait_ge(S.e_z0, 1)
    ACT.activation(T.rt[:, HC:NC], T.z0[:, HC:NC], AF.Identity, scale=T.ri[:]).then_inc(S.sc_0, 1)
    ACT.activation(cols(T.rt, 2, NC), bank(2), AF.Identity, scale=T.ri[:]).then_inc(S.sc_2, 1)

    PE.wait_ge(S.e_idy, 1)
    PE.wait_ge(S.e_z0, 1)
    PE.wait_ge(S.sc_0, 2)
    PE.matmul(bank(0), cols(T.rt, 0, NC), T.idy[:], True, True).then_inc(S.tr_0, 1)
    for b in (1, 2):
        PE.wait_ge(S["sc_%d" % b], 1)
        PE.matmul(bank(b), cols(T.rt, b, NC), T.idy[:], True, True).then_inc(S["tr_%d" % b], 1)
    PE.wait_ge(S["sc_%d" % L], 1)
    PE.matmul(T.zp[:, 512 * L:512 * L + HC], cols(T.rt, L, NC), T.idy[:, 0:HC], True, True).then_inc(S.tr_3a, 1)
    PE.matmul(T.tp[:, 0:HC], cols(T.rt, L, NC), T.idy[:, HC:NC], True, True).then_inc(S.tr_3b, 1)

    for b in (0, 1):
        ACT.wait_ge(S["tr_%d" % b], 1)
        ACT.activation(T.hb[:, b:TW:4], bank(b), AF.Copy).then_inc(S.e_h, 1)
    ACT.wait_ge(S.tr_3a, 1)
    ACT.activation(T.hb[:, L:4 * HC:4], T.zp[:, 512 * L:512 * L + HC], AF.Copy).then_inc(S.e_h, 1)
    V.wait_ge(S.tr_2, 1)
    V.tensor_copy(T.hb[:, 2:TW:4], bank(2)).then_inc(S.e_h, 1)
    V.wait_ge(S.tr_3b, 1)
    V.tensor_copy(T.hb[:, 4 * HC + L:TW:4], T.tp[:, 0:HC]).then_inc(S.e_h, 1)
    parts = G + 1

    V.wait_ge(S.e_h, parts)
    V.quantize_mx(T.hq[:], T.hs[:], T.hb[:]).then_inc(S.q_h, 1)
    V.wait_ge(S.ld_w2, 16)
    V.quantize_mx(cols(T.w2q, 0, NC), cols(T.w2s, 0, NC), cols(T.w2b, 0, TW)).then_inc(S.q_w2a, 1)
    V.quantize_mx(cols(T.w2q, 1, NC), cols(T.w2s, 1, NC), cols(T.w2b, 1, TW)).then_inc(S.q_w2b, 1)

    rid, pid, _ = topo.addr(dst)
    mask = topo.mask(core, dst)
    m_codes, m_plane = halves(mask)
    g.wait_ge(S.q_h, 1)
    g.remote_dma(T.rq[:].bitcast(dt.uint8), T.hq[:].bitcast(dt.uint8), S.arrived, S.sent, pid, rid, m_codes)
    g.remote_dma(T.rs[:], T.hs[:], S.arrived, S.sent, pid, rid, m_plane)
    g.sem_inc(S.issued, 1)
    g.wait_ge(S.sent, bin(mask).count("1"))

    SY.wait_ge(S.e_h, parts)
    SY.wait_ge(S.issued, 1)
    SY.dma_start(T.h[:], T.hb[:]).then_inc(S.st_h, 16)

    PE.wait_ge(S.q_h, 1)
    PE.wait_ge(S.q_w2a, 1)
    PE.matmul_mx(T.yp[:, 0:NC], cols(T.w2q, 0, NC), cols(T.w2s, 0, NC), T.hq[:], T.hs[:], True, False)
    PE.wait_ge(S.q_w2b, 1)
    src = T.cores[(rank + 1) % n]
    PE.wait_ge(S.arrived, bin(topo.mask(src, core)).count("1"))
    PE.matmul_mx(T.yp[:, 0:NC], cols(T.w2q, 1, NC), cols(T.w2s, 1, NC), T.rq[:], T.rs[:], False, True).then_inc(S.e_y, 1)

    V.wait_ge(S.e_y, 1)
    V.tensor_copy(T.yb[:], T.yp[:, 0:NC]).then_inc(S.e_yb, 1)
    SY.wait_ge(S.e_yb, 1)
    SY.dma_start(T.y[:], T.yb[:]).then_inc(S.st_y, 16)
    SY.wait_ge(S.st_h, 16)
    SY.wait_ge(S.st_y, 16)
